import numpy as np
import ml_dtypes


def mxq(x, axis, fmt="e4m3"):
    dtype, down = {"e4m3": (ml_dtypes.float8_e4m3fn, 7), "e5m2": (ml_dtypes.float8_e5m2, 14)}[fmt]
    v = np.moveaxis(np.asarray(x, np.float32).astype(ml_dtypes.bfloat16).astype(np.float64), axis, -1)
    blocks = v.reshape(v.shape[:-1] + (-1, 32))
    amax = np.abs(blocks).max(-1, keepdims=True)
    byte = np.maximum(np.where(amax > 0, np.frexp(amax)[1] - 1 + 127, 0) - down, 1)
    scale = np.exp2(byte - 127.0)
    codes = (blocks / scale).astype(np.float32).astype(dtype).astype(np.float64)
    return np.moveaxis((codes * scale).reshape(v.shape), -1, axis)


WIDE = False


def mx_kscale(k):
    if not WIDE:
        return np.ones(k)
    levels = np.array([10, -10, 5, -5, 0])
    if k % 512:
        return np.exp2(np.random.permutation(np.resize(levels, k // 32))).repeat(32)
    a = np.empty((k // 512, 16))
    for p in range(k // 512):
        a[p, :8] = np.random.permutation(np.resize(levels, 8))
        for g in range(8):
            far = levels[np.abs(levels - a[p, g]) >= 10]
            a[p, g + 8] = far[np.random.randint(len(far))]
    return np.exp2(a.ravel()).repeat(32)


def f64(x):
    return np.asarray(x).astype(np.float64)


def striped(idx):
    return np.tile(idx.reshape(-1, 16).T, (8, 1)).astype(np.uint16)


def unstriped(offs):
    return offs[:16].T.reshape(-1).astype(np.int64)


E2M1 = np.array([0.0, 0.5, 1.0, 1.5, 2.0, 3.0, 4.0, 6.0, -0.0, -0.5, -1.0, -1.5, -2.0, -3.0, -4.0, -6.0])


def pack_weight(w, fmt):
    k, n = w.shape
    w = f64(np.asarray(w, np.float32).astype(ml_dtypes.bfloat16)).reshape(k // 32, 32, n)
    amax = np.abs(w).max(1)
    if fmt == "e4m3":
        byte = np.frexp(amax)[1] - 1 + 127 - 7
    else:
        mant, ex = np.frexp(amax / 6.0)
        byte = np.where(mant > 0.5, ex, ex - 1) + 127
    byte = np.clip(np.where(amax > 0, byte, 1), 1, 254)
    scaled = (w * np.exp2(127.0 - byte)[:, None, :]).reshape(k, n).astype(np.float32)
    by_word = np.ascontiguousarray(scaled.reshape(k // 512, 128, 4, n).transpose(0, 1, 3, 2))
    if fmt == "e4m3":
        words = by_word.astype(ml_dtypes.float8_e4m3fn).view(np.uint8)
    else:
        c = by_word.astype(ml_dtypes.float4_e2m1fn).view(np.uint8) & 0xF
        words = (c[..., 0::2] | (c[..., 1::2] << 4)).reshape(k // 512, 128, 2 * n)
    return np.ascontiguousarray(words), np.ascontiguousarray(byte.astype(np.uint8).reshape(k // 512, 16, n))


def unpack_weight(words, scales, fmt):
    g, _, n = scales.shape
    words = np.ascontiguousarray(words).reshape(g, 128, n, -1)
    if fmt == "e4m3":
        vals = words.view(ml_dtypes.float8_e4m3fn).astype(np.float64)
    else:
        nib = np.empty((g, 128, n, 4), np.uint8)
        nib[..., 0::2] = words & 0xF
        nib[..., 1::2] = words >> 4
        vals = E2M1[nib]
    vals = vals * np.repeat(np.exp2(scales.astype(np.float64) - 127.0), 8, axis=1)[..., None]
    return vals.transpose(0, 1, 3, 2).reshape(g * 512, n)


def sigmoid(v):
    return 1.0 / (1.0 + np.exp(-np.maximum(v, -700.0)))


K, T, E, C, H, N = 512, 512, 6, 256, 512, 256
TOP = 3


def by_expert(wq, xq):
    return np.concatenate([wq[e].T @ xq[:, e * C:(e + 1) * C] for e in range(E)], axis=1)


def setup_inputs():
    n = np.random.standard_normal
    s = mx_kscale(K)[:, None]
    u = mx_kscale(H)
    deal = np.repeat(np.arange(E), C).reshape(TOP, T)[:, np.random.permutation(T)]
    deal = np.take_along_axis(deal, np.argsort(np.random.rand(TOP, T), axis=0), axis=0)
    for _ in range(8):
        s_, t_ = np.random.permutation(T).reshape(2, -1); r = np.random.randint(TOP, size=T // 2); x, y = deal[r, s_].copy(), deal[r, t_].copy()
        ok = ~((deal[:, s_] == y).any(0) | (deal[:, t_] == x).any(0)); deal[r[ok], s_[ok]] = y[ok]; deal[r[ok], t_[ok]] = x[ok]
    order = np.lexsort((np.random.rand(TOP * T), deal.reshape(-1)))
    slot_token = order % T; pos = np.empty(TOP * T, np.int64); pos[order] = np.arange(TOP * T); pos = pos.reshape(TOP, T)
    g = np.random.uniform(0.5, 1.5, (TOP, T)); g = g / g.sum(0)
    w1 = [pack_weight(m, "e2m1") for m in n((E + 1, K, H)) / np.sqrt(K) / s[None]]
    w3 = [pack_weight(m, "e2m1") for m in n((E + 1, K, H)) / np.sqrt(K) / s[None] * u[None, None, :]]
    w2 = [pack_weight(m, "e2m1") for m in n((E + 1, H, N)) / np.sqrt(H) / u[None, :, None]]
    return {
        "xT": (n((K, T)) * s).astype(np.float32),
        "w1_words": np.stack([m[0] for m in w1]),
        "w1_scales": np.stack([m[1] for m in w1]),
        "w3_words": np.stack([m[0] for m in w3]),
        "w3_scales": np.stack([m[1] for m in w3]),
        "w2_words": np.stack([m[0] for m in w2]),
        "w2_scales": np.stack([m[1] for m in w2]),
        "gate": np.stack([np.tile(r, (N, 1)) for r in g]).astype(np.float32),
        "offs": striped(slot_token),
        "pos1": striped(pos[0]),
        "pos2": striped(pos[1]),
        "pos3": striped(pos[2]),
    }


def reference(xT, w1_words, w1_scales, w3_words, w3_scales, w2_words, w2_scales, gate, offs, pos1, pos2, pos3):
    idx = unstriped(offs)
    w1 = np.stack([unpack_weight(w1_words[e], w1_scales[e], "e2m1") for e in range(E + 1)])
    w3 = np.stack([unpack_weight(w3_words[e], w3_scales[e], "e2m1") for e in range(E + 1)])
    w2 = np.stack([unpack_weight(w2_words[e], w2_scales[e], "e2m1") for e in range(E + 1)])
    w1q, w3q, w2q = w1, w3, w2
    xs = mxq(f64(xT), 0, "e4m3")
    hs = sigmoid(w1q[E].T @ xs) * (w3q[E].T @ xs)
    ys = w2q[E].T @ mxq(hs, 0, "e4m3")
    xq = mxq(f64(xT)[:, idx], 0, "e4m3")
    h = sigmoid(by_expert(w1q, xq))
    h = h * by_expert(w3q, xq)
    y = by_expert(w2q, mxq(h, 0, "e4m3"))
    return ys + sum(f64(gate[r]) * y[:, unstriped(p)] for r, p in enumerate((pos1, pos2, pos3)))

@@ -1,0 +1,225 @@
+from contextlib import ExitStack
+
+import concourse.mybir as mybir
+from concourse.masks import make_identity
+
+K, T, E, C, H, N = 512, 512, 6, 256, 512, 256
+TOP = 3
+SLOTS = E * C
+P = 128
+FLOPS = 2 * (SLOTS + T) * (2 * K * H + H * N)
+BYTES = 4 * K * T + (E + 1) * (2 * (K * H // 2 + K * H // 32) + H * N // 2 + H * N // 32) + 4 * TOP * T + 2 * P * (SLOTS + TOP * T) // 16 + 4 * N * T
+
+F32 = mybir.dt.float32
+BF16 = mybir.dt.bfloat16
+I32 = mybir.dt.int32
+U32 = mybir.dt.uint32
+U16 = mybir.dt.uint16
+U8 = mybir.dt.uint8
+FP8X4 = mybir.dt.float8_e4m3fn_x4
+FP4X4 = mybir.dt.float4_e2m1fn_x4
+MULT = mybir.AluOpType.mult
+ADD = mybir.AluOpType.add
+SIGMOID = mybir.ActivationFunctionType.Sigmoid
+
+
+def tile_moe_shr_glu_sigmoid_kernel(
+    tc, xT, w1_words, w1_scales, w3_words, w3_scales, w2_words, w2_scales, gate, offs, pos1, pos2, pos3, out
+):
+    nc = tc.nc
+    with ExitStack() as ctx:
+        keep = ctx.enter_context(tc.tile_pool(name="keep", bufs=1))
+        ring = ctx.enter_context(tc.tile_pool(name="ring", bufs=2))
+        psum = ctx.enter_context(tc.psum_pool(name="psum", bufs=2))
+
+        s1 = keep.tile([P, E + 1, H], U8, name="s1", align_bytes=64)
+        s3 = keep.tile([P, E + 1, H], U8, name="s3", align_bytes=64)
+        s2 = keep.tile([P, E + 1, N], U8, name="s2", align_bytes=64)
+        for plane in (s1, s3):
+            nc.vector.memset(plane[:].bitcast(I32), 0)
+        nc.gpsimd.memset(s2[:].bitcast(I32), 0)
+        ident = keep.tile([P, P], F32, name="ident")
+        make_identity(nc, ident[:])
+        warmed = keep.tile([P, 8], F32, name="warmed")
+        nc.scalar.activation(warmed[:], ident[:, 0:8], SIGMOID)
+
+        def load_scales(queue, plane, scales):
+            rows = scales.rearrange("e s (q r) i -> r q (e s) i", r=4)
+            for r in range(4):
+                queue.dma_start(plane[r:P:32, :, :].bitcast(I32), rows[r].bitcast(I32))
+
+        def load_words(words, first, last, name):
+            w = keep.tile([P, last - first, words.shape[3]], U8, name="%s_%d" % (name, first), align_bytes=64)
+            nc.sync.dma_start(w[:].bitcast(I32), words[first:last, 0].rearrange("e p i -> p e i").bitcast(I32))
+            return [w[:, e, :] for e in range(last - first)]
+
+        offs_sb = keep.tile([P, SLOTS // 16], U16, name="offs_sb")
+        x_rows = xT.rearrange("(p u e) t -> u p e t", u=2, e=2)
+        raw = [keep.tile([P, 2, T], F32, name="raw%d" % u) for u in range(2)]
+        nc.sync.dma_start(raw[0][:], x_rows[0])
+        nc.sync.dma_start(offs_sb[:], offs)
+        nc.sync.dma_start(raw[1][:], x_rows[1])
+        w1 = load_words(w1_words, 0, 2, "w1")
+        w3 = load_words(w3_words, 0, 2, "w3")
+        load_scales(nc.scalar, s1, w1_scales)
+        load_scales(nc.sync, s3, w3_scales)
+
+        pairs = []
+        for u in range(2):
+            xp = keep.tile([P, T, 2], BF16, name="xp%d" % u)
+            (nc.vector.tensor_copy if u == 0 else nc.scalar.copy)(xp[:], raw[u][:].rearrange("p e t -> p t e"))
+            pairs.append(xp[:].rearrange("p t e -> p (t e)").bitcast(U32))
+        planes = keep.tile([P, 2, T], I32, name="planes")
+        for u in range(2):
+            nc.sync.dma_start(planes[:, u, :], pairs[u].bitcast(I32))
+        w1 = w1 + load_words(w1_words, 2, 4, "w1")
+        w3 = w3 + load_words(w3_words, 2, 4, "w3")
+        w2 = load_words(w2_words, 0, E + 1, "w2")
+        load_scales(nc.sync, s2, w2_scales)
+        w1 = w1 + load_words(w1_words, 4, E + 1, "w1")
+        w3 = w3 + load_words(w3_words, 4, E + 1, "w3")
+        gates = keep.tile([P, TOP, T], F32, name="gates")
+        nc.sync.dma_start(gates[:], gate[:, 0:P, :].rearrange("r p t -> p r t"))
+        lists = []
+        for r, pos in enumerate((pos1, pos2, pos3)):
+            lst = keep.tile([P, T // 16], U16, name="pos%d" % r)
+            nc.sync.dma_start(lst[:], pos)
+            lists.append(lst)
+
+        y_sb = [keep.tile([P, SLOTS], F32, name="y%d" % b) for b in range(2)]
+        groups = E + T // C
+        got, xb, xq, acc, sig, h, ht, hb, hq, y = {}, {}, {}, {}, {}, {}, {}, {}, {}, {}
+
+        def quantise(src, name, bufs):
+            codes = ring.tile([P, C], U32, name=name + "_codes", bufs=bufs, align_bytes=64)
+            scales = ring.tile([P, C], U8, name=name + "_scales", bufs=bufs, align_bytes=64)
+            nc.vector.quantize_mx(codes[:].bitcast(FP8X4), scales[:], src[:])
+            return codes, scales
+
+        def gather(g, u):
+            if 0 <= g < E:
+                if u == 0:
+                    got[g] = ring.tile([P, 2, C], U32, name="got", bufs=3)
+                nc.vector.tensor_copy(got[g][:, u, :], pairs[u].indirect(offs_sb[:, g * C // 16 : (g + 1) * C // 16]))
+
+        def weave(g):
+            if 0 <= g < groups:
+                if g < E:
+                    xb[g] = ring.tile([P, 4 * C], BF16, name="xb", bufs=1, align_bytes=64)
+                    src = got[g][:]
+                else:
+                    xb[g] = ring.tile([P, 4 * C], BF16, name="xb_shared", align_bytes=64)
+                    src = planes[:, :, (g - E) * C : (g - E + 1) * C].bitcast(U32)
+                woven = xb[g][:].bitcast(U32).rearrange("p (c u) -> p c u", u=2)
+                if g in [6,7]:
+                    nc.vector.tensor_copy(woven.bitcast(I32), src.bitcast(I32).rearrange("p u c -> p c u"))
+                else:
+                    nc.scalar.copy(woven, src.rearrange("p u c -> p c u"))
+
+        def quantise_x(g):
+            if 0 <= g < groups:
+                xq[g] = quantise(xb[g], "x", 3)
+
+        def product(g, j, w, s, name, bufs):
+            if 0 <= g < groups:
+                codes, scales = xq[g]
+                cols = slice(j * P, (j + 1) * P)
+                acc[name, g, j] = psum.tile([P, H], F32, name=name, bufs=bufs)
+                nc.tensor.matmul_mx(acc[name, g, j][:], lhsT=codes[:, cols].bitcast(FP8X4), lhsT_scale=scales[:, cols],
+                                    rhs=w[min(g, E)].bitcast(FP4X4), rhs_scale=s[:, min(g, E), :], start=True, stop=True)
+
+        def sigmoid(g, j):
+            if 0 <= g < groups:
+                sig[g, j] = ring.tile([P, 2, P, 2], F32, name="sig", bufs=2)
+                nc.scalar.activation(sig[g, j][:], acc["a1", g, j][:].rearrange("c (p u d) -> c u p d", u=2, d=2), SIGMOID)
+
+        def hidden(g, j):
+            if 0 <= g < groups:
+                h[g, j] = ring.tile([P, H], BF16, name="h", bufs=4)
+                nc.vector.tensor_tensor(h[g, j][:].rearrange("c (u p d) -> c u p d", u=2, d=2),
+                                        acc["a3", g, j][:].rearrange("c (p u d) -> c u p d", u=2, d=2), sig[g, j][:], MULT)
+
+        def turn(g):
+            if 0 <= g < groups:
+                ht[g] = psum.tile([P, 2, 2, P], F32, name="ht", bufs=2)
+                for j in range(2):
+                    for u in range(2):
+                        nc.tensor.transpose(ht[g][:, j, u, :], h[g, j][:].bitcast(F32)[:, u * P : (u + 1) * P], ident[:])
+
+        def turned_out(g):
+            if 0 <= g < groups:
+                hb[g] = ring.tile([P, 4 * C], BF16, name="hb", bufs=2, align_bytes=64)
+                (nc.vector.tensor_copy if g in [] else nc.scalar.copy)(hb[g][:].bitcast(F32).rearrange("p (j c u) -> p j c u", j=2, u=2), ht[g][:].rearrange("p j u c -> p j c u"))
+
+        def quantise_h(g):
+            if 0 <= g < groups:
+                hq[g] = quantise(hb[g], "h", 2)
+
+        def second(g):
+            if 0 <= g < groups:
+                e = min(g, E)
+                codes, scales = hq[g]
+                y[g] = psum.tile([P, 2, C], F32, name="y", bufs=2)
+                for b in range(2):
+                    cols = slice(b * P, (b + 1) * P)
+                    if g < E:
+                        nc.tensor.matmul_mx(y[g][:, b, :], lhsT=w2[e][:, 2 * b * P : 2 * (b + 1) * P].bitcast(FP4X4), lhsT_scale=s2[:, e, cols],
+                                            rhs=codes[:].bitcast(FP8X4), rhs_scale=scales[:], start=True, stop=True)
+                    else:
+                        nc.tensor.matmul_mx(y[g][:, b, :], lhsT=codes[:, cols].bitcast(FP8X4), lhsT_scale=scales[:, cols],
+                                            rhs=w2[e].bitcast(FP4X4), rhs_scale=s2[:, e, :], start=True, stop=True)
+
+        shared = [keep.tile([P, 2, N], F32, name="shared%d" % half) for half in range(T // C)]
+
+        def results(g):
+            if 0 <= g < E:
+                for b in range(2):
+                    (nc.vector.tensor_copy if g in [] else nc.scalar.copy)(y_sb[b][:, g * C : (g + 1) * C], y[g][:, b, :])
+            elif E <= g < groups:
+                nc.scalar.copy(shared[g - E][:], y[g][:])
+
+        for g in range(-3, groups + 2):
+            sigmoid(g, 0)
+            product(g + 1, 0, w1, s1, "a1", 2)
+            hidden(g, 0)
+            sigmoid(g, 1)
+            product(g + 1, 1, w1, s1, "a1", 2)
+            product(g + 1, 0, w3, s3, "a3", 2)
+            hidden(g, 1)
+            product(g + 1, 1, w3, s3, "a3", 2)
+            turn(g)
+            turned_out(g - 1)
+            quantise_h(g - 1)
+            second(g - 1)
+            weave(g + 2)
+            gather(g + 3, 0)
+            quantise_x(g + 2)
+            gather(g + 3, 1)
+            results(g - 2)
+
+        def gathered(b, r, name, bufs):
+            term = ring.tile([P, T], F32, name=name, bufs=bufs)
+            nc.vector.tensor_tensor(term[:], y_sb[b][:].indirect(lists[r][:]), gates[:, r, :], MULT)
+            return term
+
+        sums = []
+        for b in range(2):
+            terms = [gathered(b, r, "term", 4) for r in range(TOP - 1)]
+            turned = psum.tile([P, T], F32, name="a1", bufs=2)
+            steps = [(n, c) for n in range(len(terms)) for c in range(T // P)]
+            for n, c in steps:
+                cols = slice(c * P, (c + 1) * P)
+                nc.tensor.matmul(turned[:, cols], terms[n][:, cols], ident[:], start=(n, c) == steps[0], stop=(n, c) == steps[-1], is_transpose=True)
+            turned_sb = ring.tile([P, T], F32, name="turned_sb")
+            nc.scalar.copy(turned_sb[:], turned[:])
+            back = psum.tile([P, T], F32, name="a3", bufs=2)
+            for c in range(T // P):
+                cols = slice(c * P, (c + 1) * P)
+                nc.tensor.matmul(back[:, cols], turned_sb[:, cols], ident[:], start=True, stop=False, is_transpose=True)
+                nc.tensor.matmul(back[:, cols], shared[c // 2][:, c % 2, b * P : (b + 1) * P], ident[:], start=False, stop=True, is_transpose=True)
+            sums.append(back)
+        for b in range(2):
+            last = gathered(b, TOP - 1, "last", 2)
+            total = ring.tile([P, T], F32, name="total")
+            nc.vector.tensor_tensor(total[:], sums[b][:], last[:], ADD)
+            nc.sync.dma_start(out[b * P : (b + 1) * P, :], total[:])

@@ -35,33 +35,34 @@ def tile_moe_shr_glu_sigmoid_kernel(
         s1 = keep.tile([P, E + 1, H], U8, name="s1", align_bytes=64)
         s3 = keep.tile([P, E + 1, H], U8, name="s3", align_bytes=64)
         s2 = keep.tile([P, E + 1, N], U8, name="s2", align_bytes=64)
-        for plane in (s1, s3):
+        for plane in (s1, s3, s2):
             nc.vector.memset(plane[:].bitcast(I32), 0)
-        nc.gpsimd.memset(s2[:].bitcast(I32), 0)
         ident = keep.tile([P, P], F32, name="ident")
         make_identity(nc, ident[:])
-        warmed = keep.tile([P, 8], F32, name="warmed")
+        warmed = keep.tile([P, 8], F32, name="warmed", align_bytes=64)
         nc.scalar.activation(warmed[:], ident[:, 0:8], SIGMOID)
 
         def load_scales(queue, plane, scales):
-            rows = scales.rearrange("e s (q r) i -> r q (e s) i", r=4)
-            for r in range(4):
-                queue.dma_start(plane[r:P:32, :, :].bitcast(I32), rows[r].bitcast(I32))
+            rows = scales.rearrange("e s (q r) i -> q r (e s) i", r=4)
+            for q in range(4):
+                queue.dma_start(plane[32 * q : 32 * q + 4, :, :].bitcast(I32), rows[q].bitcast(I32))
 
-        def load_words(words, first, last, name):
-            w = keep.tile([P, last - first, words.shape[3]], U8, name="%s_%d" % (name, first), align_bytes=64)
-            nc.sync.dma_start(w[:].bitcast(I32), words[first:last, 0].rearrange("e p i -> p e i").bitcast(I32))
-            return [w[:, e, :] for e in range(last - first)]
+        def words_tile(words, experts, name, tag=None):
+            return keep.tile([P, experts, words.shape[3]], U8, name=name, tag=tag or name, align_bytes=64)
+
+        def load_words(tile, base, words, first, last):
+            nc.sync.dma_start(tile[:, first - base : last - base, :].bitcast(I32), words[first:last, 0].rearrange("e p i -> p e i").bitcast(I32))
+            return [tile[:, e - base, :] for e in range(first, last)]
 
         offs_sb = keep.tile([P, SLOTS // 16], U16, name="offs_sb")
         x_rows = xT.rearrange("(p u e) t -> u p e t", u=2, e=2)
-        raw = [keep.tile([P, 2, T], F32, name="raw%d" % u) for u in range(2)]
+        raw = [keep.tile([P, 2, T], F32, name="raw%d" % u, align_bytes=64) for u in range(2)]
         nc.sync.dma_start(raw[0][:], x_rows[0])
         nc.sync.dma_start(offs_sb[:], offs)
         nc.sync.dma_start(raw[1][:], x_rows[1])
-        w1 = load_words(w1_words, 0, 2, "w1")
-        w3 = load_words(w3_words, 0, 2, "w3")
-        load_scales(nc.scalar, s1, w1_scales)
+        w1 = load_words(words_tile(w1_words, 2, "w1_early"), 0, w1_words, 0, 2)
+        w3 = load_words(words_tile(w3_words, 2, "w3_early"), 0, w3_words, 0, 2)
+        load_scales(nc.sync, s1, w1_scales)
         load_scales(nc.sync, s3, w3_scales)
 
         pairs = []
@@ -69,17 +70,17 @@ def tile_moe_shr_glu_sigmoid_kernel(
             xp = keep.tile([P, T, 2], BF16, name="xp%d" % u)
             (nc.vector.tensor_copy if u == 0 else nc.scalar.copy)(xp[:], raw[u][:].rearrange("p e t -> p t e"))
             pairs.append(xp[:].rearrange("p t e -> p (t e)").bitcast(U32))
+        w1_late = words_tile(w1_words, E - 1, "w1_late", "raw0")
+        w3_late = words_tile(w3_words, E - 1, "w3_late", "raw1")
+        w1 = w1 + load_words(w1_late, 2, w1_words, 2, 4)
+        w3 = w3 + load_words(w3_late, 2, w3_words, 2, 4)
+        w2 = load_words(words_tile(w2_words, E + 1, "w2", "warmed"), 0, w2_words, 0, E + 1)
+        load_scales(nc.sync, s2, w2_scales)
+        w1 = w1 + load_words(w1_late, 2, w1_words, 4, E + 1)
+        w3 = w3 + load_words(w3_late, 2, w3_words, 4, E + 1)
         planes = keep.tile([P, 2, T], I32, name="planes")
         for u in range(2):
             nc.sync.dma_start(planes[:, u, :], pairs[u].bitcast(I32))
-        w1 = w1 + load_words(w1_words, 2, 4, "w1")
-        w3 = w3 + load_words(w3_words, 2, 4, "w3")
-        w2 = load_words(w2_words, 0, E + 1, "w2")
-        load_scales(nc.sync, s2, w2_scales)
-        w1 = w1 + load_words(w1_words, 4, E + 1, "w1")
-        w3 = w3 + load_words(w3_words, 4, E + 1, "w3")
-        gates = keep.tile([P, TOP, T], F32, name="gates")
-        nc.sync.dma_start(gates[:], gate[:, 0:P, :].rearrange("r p t -> p r t"))
         lists = []
         for r, pos in enumerate((pos1, pos2, pos3)):
             lst = keep.tile([P, T // 16], U16, name="pos%d" % r)
@@ -89,6 +90,8 @@ def tile_moe_shr_glu_sigmoid_kernel(
         y_sb = [keep.tile([P, SLOTS], F32, name="y%d" % b) for b in range(2)]
         groups = E + T // C
         got, xb, xq, acc, sig, h, ht, hb, hq, y = {}, {}, {}, {}, {}, {}, {}, {}, {}, {}
+
+        both = {}
 
         def quantise(src, name, bufs):
             codes = ring.tile([P, C], U32, name=name + "_codes", bufs=bufs, align_bytes=64)
@@ -108,10 +111,10 @@ def tile_moe_shr_glu_sigmoid_kernel(
                     xb[g] = ring.tile([P, 4 * C], BF16, name="xb", bufs=1, align_bytes=64)
                     src = got[g][:]
                 else:
-                    xb[g] = ring.tile([P, 4 * C], BF16, name="xb_shared", align_bytes=64)
+                    xb[g] = ring.tile([P, 4 * C], BF16, name="xb_shared", tag="xb", bufs=1, align_bytes=64)
                     src = planes[:, :, (g - E) * C : (g - E + 1) * C].bitcast(U32)
                 woven = xb[g][:].bitcast(U32).rearrange("p (c u) -> p c u", u=2)
-                if g in [6,7]:
+                if g in [4,5,6,7]:
                     nc.vector.tensor_copy(woven.bitcast(I32), src.bitcast(I32).rearrange("p u c -> p c u"))
                 else:
                     nc.scalar.copy(woven, src.rearrange("p u c -> p c u"))
@@ -135,8 +138,10 @@ def tile_moe_shr_glu_sigmoid_kernel(
 
         def hidden(g, j):
             if 0 <= g < groups:
-                h[g, j] = ring.tile([P, H], BF16, name="h", bufs=4)
-                nc.vector.tensor_tensor(h[g, j][:].rearrange("c (u p d) -> c u p d", u=2, d=2),
+                if j == 0:
+                    both[g] = ring.tile([P, 2, H], BF16, name="hh", bufs=3)
+                h[g, j] = both[g][:, j, :]
+                nc.vector.tensor_tensor(h[g, j].rearrange("c (u p d) -> c u p d", u=2, d=2),
                                         acc["a3", g, j][:].rearrange("c (p u d) -> c u p d", u=2, d=2), sig[g, j][:], MULT)
 
         def turn(g):
@@ -144,7 +149,7 @@ def tile_moe_shr_glu_sigmoid_kernel(
                 ht[g] = psum.tile([P, 2, 2, P], F32, name="ht", bufs=2)
                 for j in range(2):
                     for u in range(2):
-                        nc.tensor.transpose(ht[g][:, j, u, :], h[g, j][:].bitcast(F32)[:, u * P : (u + 1) * P], ident[:])
+                        nc.tensor.transpose(ht[g][:, j, u, :], h[g, j].bitcast(F32)[:, u * P : (u + 1) * P], ident[:])
 
         def turned_out(g):
             if 0 <= g < groups:
@@ -180,22 +185,25 @@ def tile_moe_shr_glu_sigmoid_kernel(
 
         for g in range(-3, groups + 2):
             sigmoid(g, 0)
-            product(g + 1, 0, w1, s1, "a1", 2)
             hidden(g, 0)
             sigmoid(g, 1)
+            hidden(g, 1)
+            turn(g)
+            product(g + 1, 0, w1, s1, "a1", 2)
             product(g + 1, 1, w1, s1, "a1", 2)
             product(g + 1, 0, w3, s3, "a3", 2)
-            hidden(g, 1)
             product(g + 1, 1, w3, s3, "a3", 2)
-            turn(g)
             turned_out(g - 1)
             quantise_h(g - 1)
             second(g - 1)
-            weave(g + 2)
-            gather(g + 3, 0)
-            quantise_x(g + 2)
-            gather(g + 3, 1)
             results(g - 2)
+            weave(g + 2)
+            quantise_x(g + 2)
+            gather(g + 3, 0)
+            gather(g + 3, 1)
+
+        gates = keep.tile([P, TOP, T], F32, name="gates", tag="planes")
+        nc.sync.dma_start(gates[:], gate[:, 0:P, :].rearrange("r p t -> p r t"))
 
         def gathered(b, r, name, bufs):
             term = ring.tile([P, T], F32, name=name, bufs=bufs)
@@ -214,9 +222,10 @@ def tile_moe_shr_glu_sigmoid_kernel(
             nc.scalar.copy(turned_sb[:], turned[:])
             back = psum.tile([P, T], F32, name="a3", bufs=2)
             for c in range(T // P):
+                nc.tensor.matmul(back[:, c * P : (c + 1) * P], shared[c // 2][:, c % 2, b * P : (b + 1) * P], ident[:], start=c == 0, stop=False, is_transpose=True)
+            for c in range(T // P):
                 cols = slice(c * P, (c + 1) * P)
-                nc.tensor.matmul(back[:, cols], turned_sb[:, cols], ident[:], start=True, stop=False, is_transpose=True)
-                nc.tensor.matmul(back[:, cols], shared[c // 2][:, c % 2, b * P : (b + 1) * P], ident[:], start=False, stop=True, is_transpose=True)
+                nc.tensor.matmul(back[:, cols], turned_sb[:, cols], ident[:], start=False, stop=c == T // P - 1, is_transpose=True)
             sums.append(back)
         for b in range(2):
             last = gathered(b, TOP - 1, "last", 2)

@@ -6,9 +6,23 @@ from concourse.masks import make_identity
 K, T, E, C, H, N = 512, 512, 6, 256, 512, 256
 TOP = 3
 SLOTS = E * C
+GROUPS = E + T // C
 P = 128
 FLOPS = 2 * (SLOTS + T) * (2 * K * H + H * N)
-BYTES = 4 * K * T + (E + 1) * (2 * (K * H // 2 + K * H // 32) + H * N // 2 + H * N // 32) + 4 * TOP * T + 2 * P * (SLOTS + TOP * T) // 16 + 4 * N * T
+BYTES = (
+    4 * K * T
+    + (E + 1) * (2 * (K * H // 2 + K * H // 32) + H * N // 2 + H * N // 32)
+    + 4 * TOP * T
+    + 2 * P * (SLOTS + TOP * T) // 16
+    + 4 * N * T
+)
+
+CAST_SPLIT = 384
+EARLY, MID = 2, 4
+WEAVE_ON_VECTOR_FROM = 4
+RESULTS_ON_VECTOR = (3, 4)
+BANKS = {"a1": 2, "a3": 3, "h_turned": 1, "y": 2}
+GATHER_BUFS, SIGMOID_BUFS, HIDDEN_BUFS = 3, 4, 3
 
 F32 = mybir.dt.float32
 BF16 = mybir.dt.bfloat16
@@ -35,7 +49,7 @@ def tile_moe_shr_glu_sigmoid_kernel(
         s1 = keep.tile([P, E + 1, H], U8, name="s1", align_bytes=64)
         s3 = keep.tile([P, E + 1, H], U8, name="s3", align_bytes=64)
         s2 = keep.tile([P, E + 1, N], U8, name="s2", align_bytes=64)
-        for plane in (s1, s3, s2):
+        for plane in (s3, s1, s2):
             nc.vector.memset(plane[:].bitcast(I32), 0)
         ident = keep.tile([P, P], F32, name="ident")
         make_identity(nc, ident[:])
@@ -43,192 +57,219 @@ def tile_moe_shr_glu_sigmoid_kernel(
         nc.scalar.activation(warmed[:], ident[:, 0:8], SIGMOID)
 
         def load_scales(queue, plane, scales):
-            rows = scales.rearrange("e s (q r) i -> q r (e s) i", r=4)
-            for q in range(4):
-                queue.dma_start(plane[32 * q : 32 * q + 4, :, :].bitcast(I32), rows[q].bitcast(I32))
+            rows = scales.rearrange("e s (quad r) i -> quad r (e s) i", r=4)
+            for quad in range(4):
+                queue.dma_start(plane[32 * quad : 32 * quad + 4, :, :].bitcast(I32), rows[quad].bitcast(I32))
 
-        def words_tile(words, experts, name, tag=None):
-            return keep.tile([P, experts, words.shape[3]], U8, name=name, tag=tag or name, align_bytes=64)
+        def load_words(words, first, last, name, tag):
+            tile = keep.tile([P, last - first, words.shape[3]], U8, name=name, tag=tag, align_bytes=64)
+            nc.sync.dma_start(tile[:].bitcast(I32), words[first:last, 0].rearrange("e p i -> p e i").bitcast(I32))
+            return [tile[:, e, :] for e in range(last - first)]
 
-        def load_words(tile, base, words, first, last):
-            nc.sync.dma_start(tile[:, first - base : last - base, :].bitcast(I32), words[first:last, 0].rearrange("e p i -> p e i").bitcast(I32))
-            return [tile[:, e - base, :] for e in range(first, last)]
+        x_rows = xT.rearrange("(p u d) t -> u p d t", u=2, d=2)
+
+        def load_x(u, cols, name):
+            tile = keep.tile([P, 2, cols.stop - cols.start], F32, name=name, align_bytes=64)
+            nc.sync.dma_start(tile[:], x_rows[u][:, :, cols])
+            return tile
 
         offs_sb = keep.tile([P, SLOTS // 16], U16, name="offs_sb")
-        x_rows = xT.rearrange("(p u e) t -> u p e t", u=2, e=2)
-        raw = [keep.tile([P, 2, T], F32, name="raw%d" % u, align_bytes=64) for u in range(2)]
-        nc.sync.dma_start(raw[0][:], x_rows[0])
+        left, right = slice(0, CAST_SPLIT), slice(CAST_SPLIT, T)
+        raw_left = load_x(0, left, "raw_left")
+        raw_right = load_x(0, right, "raw_right")
         nc.sync.dma_start(offs_sb[:], offs)
-        nc.sync.dma_start(raw[1][:], x_rows[1])
-        w1 = load_words(words_tile(w1_words, 2, "w1_early"), 0, w1_words, 0, 2)
-        w3 = load_words(words_tile(w3_words, 2, "w3_early"), 0, w3_words, 0, 2)
+        raw_high = load_x(1, slice(0, T), "raw_high")
+        w1 = load_words(w1_words, 0, EARLY, "w1_early", "w1_early")
         load_scales(nc.sync, s1, w1_scales)
-        load_scales(nc.sync, s3, w3_scales)
+        w3 = load_words(w3_words, 0, EARLY, "w3_early", "w3_early")
+        load_scales(nc.gpsimd, s3, w3_scales)
 
-        pairs = []
-        for u in range(2):
-            xp = keep.tile([P, T, 2], BF16, name="xp%d" % u)
-            (nc.vector.tensor_copy if u == 0 else nc.scalar.copy)(xp[:], raw[u][:].rearrange("p e t -> p t e"))
-            pairs.append(xp[:].rearrange("p t e -> p (t e)").bitcast(U32))
-        w1_late = words_tile(w1_words, E - 1, "w1_late", "raw0")
-        w3_late = words_tile(w3_words, E - 1, "w3_late", "raw1")
-        w1 = w1 + load_words(w1_late, 2, w1_words, 2, 4)
-        w3 = w3 + load_words(w3_late, 2, w3_words, 2, 4)
-        w2 = load_words(words_tile(w2_words, E + 1, "w2", "warmed"), 0, w2_words, 0, E + 1)
+        x_bf = [keep.tile([P, T, 2], BF16, name="x_bf%d" % u) for u in range(2)]
+        nc.vector.tensor_copy(x_bf[0][:, left, :], raw_left[:].rearrange("p d t -> p t d"))
+        nc.scalar.copy(x_bf[0][:, right, :], raw_right[:].rearrange("p d t -> p t d"))
+        nc.scalar.copy(x_bf[1][:], raw_high[:].rearrange("p d t -> p t d"))
+        pairs = [tile[:].rearrange("p t d -> p (t d)").bitcast(U32) for tile in x_bf]
+
+        w1 = w1 + load_words(w1_words, EARLY, MID, "w1_mid", "raw_left")
+        w3 = w3 + load_words(w3_words, EARLY, MID, "w3_mid", "raw_high")
+        w2 = load_words(w2_words, 0, E + 1, "w2", "raw_right")
         load_scales(nc.sync, s2, w2_scales)
-        w1 = w1 + load_words(w1_late, 2, w1_words, 4, E + 1)
-        w3 = w3 + load_words(w3_late, 2, w3_words, 4, E + 1)
-        planes = keep.tile([P, 2, T], I32, name="planes")
+        w1 = w1 + load_words(w1_words, MID, E + 1, "w1_end", "w1_early")
+        w3 = w3 + load_words(w3_words, MID, E + 1, "w3_end", "w3_early")
+        all_pairs = keep.tile([P, 2, T], I32, name="all_pairs")
         for u in range(2):
-            nc.sync.dma_start(planes[:, u, :], pairs[u].bitcast(I32))
-        lists = []
+            nc.sync.dma_start(all_pairs[:, u, :], pairs[u].bitcast(I32))
+        pos_sb = []
         for r, pos in enumerate((pos1, pos2, pos3)):
-            lst = keep.tile([P, T // 16], U16, name="pos%d" % r)
-            nc.sync.dma_start(lst[:], pos)
-            lists.append(lst)
+            pos_tile = keep.tile([P, T // 16], U16, name="pos%d" % r)
+            nc.sync.dma_start(pos_tile[:], pos)
+            pos_sb.append(pos_tile)
 
         y_sb = [keep.tile([P, SLOTS], F32, name="y%d" % b) for b in range(2)]
-        groups = E + T // C
-        got, xb, xq, acc, sig, h, ht, hb, hq, y = {}, {}, {}, {}, {}, {}, {}, {}, {}, {}
+        gathered_pairs, x_woven, x_mx, first_sums, sig, h, h_turned, h_woven, h_mx, y = [{} for n in range(10)]
 
-        both = {}
-
-        def quantise(src, name, bufs):
-            codes = ring.tile([P, C], U32, name=name + "_codes", bufs=bufs, align_bytes=64)
-            scales = ring.tile([P, C], U8, name=name + "_scales", bufs=bufs, align_bytes=64)
+        def quantise(src, name):
+            codes = ring.tile([P, C], U32, name=name + "_codes", align_bytes=64)
+            scales = ring.tile([P, C], U8, name=name + "_scales", align_bytes=64)
             nc.vector.quantize_mx(codes[:].bitcast(FP8X4), scales[:], src[:])
             return codes, scales
 
         def gather(g, u):
             if 0 <= g < E:
                 if u == 0:
-                    got[g] = ring.tile([P, 2, C], U32, name="got", bufs=3)
-                nc.vector.tensor_copy(got[g][:, u, :], pairs[u].indirect(offs_sb[:, g * C // 16 : (g + 1) * C // 16]))
+                    gathered_pairs[g] = ring.tile([P, 2, C], U32, name="gathered_pairs", bufs=GATHER_BUFS, align_bytes=64)
+                entries = offs_sb[:, g * C // 16 : (g + 1) * C // 16]
+                nc.vector.tensor_copy(gathered_pairs[g][:, u, :], pairs[u].indirect(entries))
 
         def weave(g):
-            if 0 <= g < groups:
+            if 0 <= g < GROUPS:
+                x_woven[g] = ring.tile([P, 4 * C], BF16, name="x_woven", align_bytes=64)
                 if g < E:
-                    xb[g] = ring.tile([P, 4 * C], BF16, name="xb", bufs=1, align_bytes=64)
-                    src = got[g][:]
+                    src = gathered_pairs[g][:]
                 else:
-                    xb[g] = ring.tile([P, 4 * C], BF16, name="xb_shared", tag="xb", bufs=1, align_bytes=64)
-                    src = planes[:, :, (g - E) * C : (g - E + 1) * C].bitcast(U32)
-                woven = xb[g][:].bitcast(U32).rearrange("p (c u) -> p c u", u=2)
-                if g in [4,5,6,7]:
-                    nc.vector.tensor_copy(woven.bitcast(I32), src.bitcast(I32).rearrange("p u c -> p c u"))
+                    src = all_pairs[:, :, (g - E) * C : (g - E + 1) * C].bitcast(U32)
+                dst = x_woven[g][:].bitcast(U32).rearrange("p (c u) -> p c u", u=2)
+                if g >= WEAVE_ON_VECTOR_FROM:
+                    nc.vector.tensor_copy(dst.bitcast(I32), src.bitcast(I32).rearrange("p u c -> p c u"))
                 else:
-                    nc.scalar.copy(woven, src.rearrange("p u c -> p c u"))
+                    nc.scalar.copy(dst, src.rearrange("p u c -> p c u"))
 
         def quantise_x(g):
-            if 0 <= g < groups:
-                xq[g] = quantise(xb[g], "x", 3)
+            if 0 <= g < GROUPS:
+                x_mx[g] = quantise(x_woven[g], "x")
 
-        def product(g, j, w, s, name, bufs):
-            if 0 <= g < groups:
-                codes, scales = xq[g]
+        def first_product(g, j, words, plane, bank):
+            if 0 <= g < GROUPS:
+                codes, scales = x_mx[g]
                 cols = slice(j * P, (j + 1) * P)
-                acc[name, g, j] = psum.tile([P, H], F32, name=name, bufs=bufs)
-                nc.tensor.matmul_mx(acc[name, g, j][:], lhsT=codes[:, cols].bitcast(FP8X4), lhsT_scale=scales[:, cols],
-                                    rhs=w[min(g, E)].bitcast(FP4X4), rhs_scale=s[:, min(g, E), :], start=True, stop=True)
+                e = min(g, E)
+                first_sums[bank, g, j] = psum.tile([P, H], F32, name=bank, bufs=BANKS[bank])
+                nc.tensor.matmul_mx(
+                    first_sums[bank, g, j][:],
+                    lhsT=codes[:, cols].bitcast(FP8X4),
+                    lhsT_scale=scales[:, cols],
+                    rhs=words[e].bitcast(FP4X4),
+                    rhs_scale=plane[:, e, :],
+                    start=True,
+                    stop=True,
+                )
+
+        def by_pair(bank):
+            return bank[:].rearrange("c (p u d) -> c u p d", u=2, d=2)
 
         def sigmoid(g, j):
-            if 0 <= g < groups:
-                sig[g, j] = ring.tile([P, 2, P, 2], F32, name="sig", bufs=2)
-                nc.scalar.activation(sig[g, j][:], acc["a1", g, j][:].rearrange("c (p u d) -> c u p d", u=2, d=2), SIGMOID)
+            if 0 <= g < GROUPS:
+                sig[g, j] = ring.tile([P, 2, P, 2], F32, name="sig", bufs=SIGMOID_BUFS, align_bytes=64)
+                nc.scalar.activation(sig[g, j][:], by_pair(first_sums["a1", g, j]), SIGMOID)
 
         def hidden(g, j):
-            if 0 <= g < groups:
+            if 0 <= g < GROUPS:
                 if j == 0:
-                    both[g] = ring.tile([P, 2, H], BF16, name="hh", bufs=3)
-                h[g, j] = both[g][:, j, :]
-                nc.vector.tensor_tensor(h[g, j].rearrange("c (u p d) -> c u p d", u=2, d=2),
-                                        acc["a3", g, j][:].rearrange("c (p u d) -> c u p d", u=2, d=2), sig[g, j][:], MULT)
+                    h[g] = ring.tile([P, 2, H], BF16, name="h", bufs=HIDDEN_BUFS, align_bytes=64)
+                dst = h[g][:, j, :].rearrange("c (u p d) -> c u p d", u=2, d=2)
+                nc.vector.tensor_tensor(dst, by_pair(first_sums["a3", g, j]), sig[g, j][:], MULT)
 
         def turn(g):
-            if 0 <= g < groups:
-                ht[g] = psum.tile([P, 2, 2, P], F32, name="ht", bufs=2)
+            if 0 <= g < GROUPS:
+                h_turned[g] = psum.tile([P, 2, 2, P], F32, name="h_turned", bufs=BANKS["h_turned"])
                 for j in range(2):
                     for u in range(2):
-                        nc.tensor.transpose(ht[g][:, j, u, :], h[g, j].bitcast(F32)[:, u * P : (u + 1) * P], ident[:])
+                        h_pairs = h[g][:, j, :].bitcast(F32)[:, u * P : (u + 1) * P]
+                        nc.tensor.transpose(h_turned[g][:, j, u, :], h_pairs, ident[:])
 
-        def turned_out(g):
-            if 0 <= g < groups:
-                hb[g] = ring.tile([P, 4 * C], BF16, name="hb", bufs=2, align_bytes=64)
-                (nc.vector.tensor_copy if g in [] else nc.scalar.copy)(hb[g][:].bitcast(F32).rearrange("p (j c u) -> p j c u", j=2, u=2), ht[g][:].rearrange("p j u c -> p j c u"))
+        def weave_h(g):
+            if 0 <= g < GROUPS:
+                h_woven[g] = ring.tile([P, 4 * C], BF16, name="h_woven", align_bytes=64)
+                dst = h_woven[g][:].bitcast(F32).rearrange("p (j c u) -> p j c u", j=2, u=2)
+                nc.scalar.copy(dst, h_turned[g][:].rearrange("p j u c -> p j c u"))
 
         def quantise_h(g):
-            if 0 <= g < groups:
-                hq[g] = quantise(hb[g], "h", 2)
+            if 0 <= g < GROUPS:
+                h_mx[g] = quantise(h_woven[g], "h")
 
-        def second(g):
-            if 0 <= g < groups:
+        def second_product(g):
+            if 0 <= g < GROUPS:
                 e = min(g, E)
-                codes, scales = hq[g]
-                y[g] = psum.tile([P, 2, C], F32, name="y", bufs=2)
+                codes, scales = h_mx[g]
+                y[g] = psum.tile([P, 2, C], F32, name="y", bufs=BANKS["y"])
                 for b in range(2):
                     cols = slice(b * P, (b + 1) * P)
                     if g < E:
-                        nc.tensor.matmul_mx(y[g][:, b, :], lhsT=w2[e][:, 2 * b * P : 2 * (b + 1) * P].bitcast(FP4X4), lhsT_scale=s2[:, e, cols],
-                                            rhs=codes[:].bitcast(FP8X4), rhs_scale=scales[:], start=True, stop=True)
+                        nc.tensor.matmul_mx(
+                            y[g][:, b, :],
+                            lhsT=w2[e][:, 2 * b * P : 2 * (b + 1) * P].bitcast(FP4X4),
+                            lhsT_scale=s2[:, e, cols],
+                            rhs=codes[:].bitcast(FP8X4),
+                            rhs_scale=scales[:],
+                            start=True,
+                            stop=True,
+                        )
                     else:
-                        nc.tensor.matmul_mx(y[g][:, b, :], lhsT=codes[:, cols].bitcast(FP8X4), lhsT_scale=scales[:, cols],
-                                            rhs=w2[e].bitcast(FP4X4), rhs_scale=s2[:, e, :], start=True, stop=True)
+                        nc.tensor.matmul_mx(
+                            y[g][:, b, :],
+                            lhsT=codes[:, cols].bitcast(FP8X4),
+                            lhsT_scale=scales[:, cols],
+                            rhs=w2[e].bitcast(FP4X4),
+                            rhs_scale=s2[:, e, :],
+                            start=True,
+                            stop=True,
+                        )
 
         shared = [keep.tile([P, 2, N], F32, name="shared%d" % half) for half in range(T // C)]
 
-        def results(g):
+        def results_out(g):
             if 0 <= g < E:
+                move = nc.vector.tensor_copy if g in RESULTS_ON_VECTOR else nc.scalar.copy
                 for b in range(2):
-                    (nc.vector.tensor_copy if g in [] else nc.scalar.copy)(y_sb[b][:, g * C : (g + 1) * C], y[g][:, b, :])
-            elif E <= g < groups:
+                    move(y_sb[b][:, g * C : (g + 1) * C], y[g][:, b, :])
+            elif E <= g < GROUPS:
                 nc.scalar.copy(shared[g - E][:], y[g][:])
 
-        for g in range(-3, groups + 2):
-            sigmoid(g, 0)
-            hidden(g, 0)
-            sigmoid(g, 1)
-            hidden(g, 1)
+        for g in range(-3, GROUPS + 2):
+            for j in range(2):
+                sigmoid(g, j)
+                hidden(g, j)
             turn(g)
-            product(g + 1, 0, w1, s1, "a1", 2)
-            product(g + 1, 1, w1, s1, "a1", 2)
-            product(g + 1, 0, w3, s3, "a3", 2)
-            product(g + 1, 1, w3, s3, "a3", 2)
-            turned_out(g - 1)
+            for words, plane, bank in ((w1, s1, "a1"), (w3, s3, "a3")):
+                for j in range(2):
+                    first_product(g + 1, j, words, plane, bank)
+            weave_h(g - 1)
             quantise_h(g - 1)
-            second(g - 1)
-            results(g - 2)
+            second_product(g - 1)
+            results_out(g - 2)
             weave(g + 2)
             quantise_x(g + 2)
-            gather(g + 3, 0)
-            gather(g + 3, 1)
+            for u in range(2):
+                gather(g + 3, u)
 
-        gates = keep.tile([P, TOP, T], F32, name="gates", tag="planes")
+        gates = keep.tile([P, TOP, T], F32, name="gates", tag="raw_left", align_bytes=64)
         nc.sync.dma_start(gates[:], gate[:, 0:P, :].rearrange("r p t -> p r t"))
 
-        def gathered(b, r, name, bufs):
+        def gated_term(b, r, name, bufs):
             term = ring.tile([P, T], F32, name=name, bufs=bufs)
-            nc.vector.tensor_tensor(term[:], y_sb[b][:].indirect(lists[r][:]), gates[:, r, :], MULT)
-            return term
+            nc.vector.tensor_tensor(term[:], y_sb[b][:].indirect(pos_sb[r][:]), gates[:, r, :], MULT)
+            return term[:]
 
-        sums = []
+        chunks = [slice(c * P, (c + 1) * P) for c in range(T // P)]
+        partial = []
         for b in range(2):
-            terms = [gathered(b, r, "term", 4) for r in range(TOP - 1)]
-            turned = psum.tile([P, T], F32, name="a1", bufs=2)
-            steps = [(n, c) for n in range(len(terms)) for c in range(T // P)]
-            for n, c in steps:
-                cols = slice(c * P, (c + 1) * P)
-                nc.tensor.matmul(turned[:, cols], terms[n][:, cols], ident[:], start=(n, c) == steps[0], stop=(n, c) == steps[-1], is_transpose=True)
+            terms = [gated_term(b, r, "term", 2 * (TOP - 1)) for r in range(TOP - 1)]
+            turned = psum.tile([P, T], F32, name="a1", bufs=BANKS["a1"])
+            steps = [(term, cols) for term in terms for cols in chunks]
+            for n, (term, cols) in enumerate(steps):
+                nc.tensor.matmul(turned[:, cols], term[:, cols], ident[:], start=n == 0, stop=n == len(steps) - 1, is_transpose=True)
             turned_sb = ring.tile([P, T], F32, name="turned_sb")
             nc.scalar.copy(turned_sb[:], turned[:])
-            back = psum.tile([P, T], F32, name="a3", bufs=2)
-            for c in range(T // P):
-                nc.tensor.matmul(back[:, c * P : (c + 1) * P], shared[c // 2][:, c % 2, b * P : (b + 1) * P], ident[:], start=c == 0, stop=False, is_transpose=True)
-            for c in range(T // P):
-                cols = slice(c * P, (c + 1) * P)
-                nc.tensor.matmul(back[:, cols], turned_sb[:, cols], ident[:], start=False, stop=c == T // P - 1, is_transpose=True)
-            sums.append(back)
+            back = psum.tile([P, T], F32, name="a3", bufs=BANKS["a3"])
+            steps = [(shared[c // 2][:, c % 2, b * P : (b + 1) * P], cols) for c, cols in enumerate(chunks)]
+            steps = steps + [(turned_sb[:, cols], cols) for cols in chunks]
+            for n, (src, cols) in enumerate(steps):
+                nc.tensor.matmul(back[:, cols], src, ident[:], start=n == 0, stop=n == len(steps) - 1, is_transpose=True)
+            partial.append(back)
+
         for b in range(2):
-            last = gathered(b, TOP - 1, "last", 2)
+            last = gated_term(b, TOP - 1, "last", 2)
             total = ring.tile([P, T], F32, name="total")
-            nc.vector.tensor_tensor(total[:], sums[b][:], last[:], ADD)
-            nc.sync.dma_start(out[b * P : (b + 1) * P, :], total[:])
+            for cols in [slice(0, T)] if b == 0 else [slice(0, T // 2), slice(T // 2, T)]:
+                nc.vector.tensor_tensor(total[:, cols], partial[b][:, cols], last[:, cols], ADD)
+                nc.sync.dma_start(out[b * P : (b + 1) * P, cols], total[:, cols])

from contextlib import ExitStack

import concourse.mybir as mybir
from concourse.masks import make_identity

K, T, E, C, H, N = 512, 512, 6, 256, 512, 256
TOP = 3
SLOTS = E * C
GROUPS = E + T // C
P = 128
FLOPS = 2 * (SLOTS + T) * (2 * K * H + H * N)
BYTES = (
    4 * K * T
    + (E + 1) * (2 * (K * H // 2 + K * H // 32) + H * N // 2 + H * N // 32)
    + 4 * TOP * T
    + 2 * P * (SLOTS + TOP * T) // 16
    + 4 * N * T
)

CAST_SPLIT = 384
EARLY, MID = 2, 4
WEAVE_ON_VECTOR_FROM = 4
RESULTS_ON_VECTOR = (3, 4)
BANKS = {"a1": 2, "a3": 3, "h_turned": 1, "y": 2}
GATHER_BUFS, SIGMOID_BUFS, HIDDEN_BUFS = 3, 4, 3

F32 = mybir.dt.float32
BF16 = mybir.dt.bfloat16
I32 = mybir.dt.int32
U32 = mybir.dt.uint32
U16 = mybir.dt.uint16
U8 = mybir.dt.uint8
FP8X4 = mybir.dt.float8_e4m3fn_x4
FP4X4 = mybir.dt.float4_e2m1fn_x4
MULT = mybir.AluOpType.mult
ADD = mybir.AluOpType.add
SIGMOID = mybir.ActivationFunctionType.Sigmoid


def tile_moe_shr_glu_sigmoid_kernel(
    tc, xT, w1_words, w1_scales, w3_words, w3_scales, w2_words, w2_scales, gate, offs, pos1, pos2, pos3, out
):
    nc = tc.nc
    with ExitStack() as ctx:
        keep = ctx.enter_context(tc.tile_pool(name="keep", bufs=1))
        ring = ctx.enter_context(tc.tile_pool(name="ring", bufs=2))
        psum = ctx.enter_context(tc.psum_pool(name="psum", bufs=2))

        s1 = keep.tile([P, E + 1, H], U8, name="s1", align_bytes=64)
        s3 = keep.tile([P, E + 1, H], U8, name="s3", align_bytes=64)
        s2 = keep.tile([P, E + 1, N], U8, name="s2", align_bytes=64)
        for plane in (s3, s1, s2):
            nc.vector.memset(plane[:].bitcast(I32), 0)
        ident = keep.tile([P, P], F32, name="ident")
        make_identity(nc, ident[:])
        warmed = keep.tile([P, 8], F32, name="warmed", align_bytes=64)
        nc.scalar.activation(warmed[:], ident[:, 0:8], SIGMOID)

        def load_scales(queue, plane, scales):
            rows = scales.rearrange("e s (quad r) i -> quad r (e s) i", r=4)
            for quad in range(4):
                queue.dma_start(plane[32 * quad : 32 * quad + 4, :, :].bitcast(I32), rows[quad].bitcast(I32))

        def load_words(words, first, last, name, tag):
            tile = keep.tile([P, last - first, words.shape[3]], U8, name=name, tag=tag, align_bytes=64)
            nc.sync.dma_start(tile[:].bitcast(I32), words[first:last, 0].rearrange("e p i -> p e i").bitcast(I32))
            return [tile[:, e, :] for e in range(last - first)]

        x_rows = xT.rearrange("(p u d) t -> u p d t", u=2, d=2)

        def load_x(u, cols, name):
            tile = keep.tile([P, 2, cols.stop - cols.start], F32, name=name, align_bytes=64)
            nc.sync.dma_start(tile[:], x_rows[u][:, :, cols])
            return tile

        offs_sb = keep.tile([P, SLOTS // 16], U16, name="offs_sb")
        left, right = slice(0, CAST_SPLIT), slice(CAST_SPLIT, T)
        raw_left = load_x(0, left, "raw_left")
        raw_right = load_x(0, right, "raw_right")
        nc.sync.dma_start(offs_sb[:], offs)
        raw_high = load_x(1, slice(0, T), "raw_high")
        w1 = load_words(w1_words, 0, EARLY, "w1_early", "w1_early")
        load_scales(nc.sync, s1, w1_scales)
        w3 = load_words(w3_words, 0, EARLY, "w3_early", "w3_early")
        load_scales(nc.gpsimd, s3, w3_scales)

        x_bf = [keep.tile([P, T, 2], BF16, name="x_bf%d" % u) for u in range(2)]
        nc.vector.tensor_copy(x_bf[0][:, left, :], raw_left[:].rearrange("p d t -> p t d"))
        nc.scalar.copy(x_bf[0][:, right, :], raw_right[:].rearrange("p d t -> p t d"))
        nc.scalar.copy(x_bf[1][:], raw_high[:].rearrange("p d t -> p t d"))
        pairs = [tile[:].rearrange("p t d -> p (t d)").bitcast(U32) for tile in x_bf]

        w1 = w1 + load_words(w1_words, EARLY, MID, "w1_mid", "raw_left")
        w3 = w3 + load_words(w3_words, EARLY, MID, "w3_mid", "raw_high")
        w2 = load_words(w2_words, 0, E + 1, "w2", "raw_right")
        load_scales(nc.sync, s2, w2_scales)
        w1 = w1 + load_words(w1_words, MID, E + 1, "w1_end", "w1_early")
        w3 = w3 + load_words(w3_words, MID, E + 1, "w3_end", "w3_early")
        all_pairs = keep.tile([P, 2, T], I32, name="all_pairs")
        for u in range(2):
            nc.sync.dma_start(all_pairs[:, u, :], pairs[u].bitcast(I32))
        pos_sb = []
        for r, pos in enumerate((pos1, pos2, pos3)):
            pos_tile = keep.tile([P, T // 16], U16, name="pos%d" % r)
            nc.sync.dma_start(pos_tile[:], pos)
            pos_sb.append(pos_tile)

        y_sb = [keep.tile([P, SLOTS], F32, name="y%d" % b) for b in range(2)]
        gathered_pairs, x_woven, x_mx, first_sums, sig, h, h_turned, h_woven, h_mx, y = [{} for n in range(10)]

        def quantise(src, name):
            codes = ring.tile([P, C], U32, name=name + "_codes", align_bytes=64)
            scales = ring.tile([P, C], U8, name=name + "_scales", align_bytes=64)
            nc.vector.quantize_mx(codes[:].bitcast(FP8X4), scales[:], src[:])
            return codes, scales

        def gather(g, u):
            if 0 <= g < E:
                if u == 0:
                    gathered_pairs[g] = ring.tile([P, 2, C], U32, name="gathered_pairs", bufs=GATHER_BUFS, align_bytes=64)
                entries = offs_sb[:, g * C // 16 : (g + 1) * C // 16]
                nc.vector.tensor_copy(gathered_pairs[g][:, u, :], pairs[u].indirect(entries))

        def weave(g):
            if 0 <= g < GROUPS:
                x_woven[g] = ring.tile([P, 4 * C], BF16, name="x_woven", align_bytes=64)
                if g < E:
                    src = gathered_pairs[g][:]
                else:
                    src = all_pairs[:, :, (g - E) * C : (g - E + 1) * C].bitcast(U32)
                dst = x_woven[g][:].bitcast(U32).rearrange("p (c u) -> p c u", u=2)
                if g >= WEAVE_ON_VECTOR_FROM:
                    nc.vector.tensor_copy(dst.bitcast(I32), src.bitcast(I32).rearrange("p u c -> p c u"))
                else:
                    nc.scalar.copy(dst, src.rearrange("p u c -> p c u"))

        def quantise_x(g):
            if 0 <= g < GROUPS:
                x_mx[g] = quantise(x_woven[g], "x")

        def first_product(g, j, words, plane, bank):
            if 0 <= g < GROUPS:
                codes, scales = x_mx[g]
                cols = slice(j * P, (j + 1) * P)
                e = min(g, E)
                first_sums[bank, g, j] = psum.tile([P, H], F32, name=bank, bufs=BANKS[bank])
                nc.tensor.matmul_mx(
                    first_sums[bank, g, j][:],
                    lhsT=codes[:, cols].bitcast(FP8X4),
                    lhsT_scale=scales[:, cols],
                    rhs=words[e].bitcast(FP4X4),
                    rhs_scale=plane[:, e, :],
                    start=True,
                    stop=True,
                )

        def by_pair(bank):
            return bank[:].rearrange("c (p u d) -> c u p d", u=2, d=2)

        def sigmoid(g, j):
            if 0 <= g < GROUPS:
                sig[g, j] = ring.tile([P, 2, P, 2], F32, name="sig", bufs=SIGMOID_BUFS, align_bytes=64)
                nc.scalar.activation(sig[g, j][:], by_pair(first_sums["a1", g, j]), SIGMOID)

        def hidden(g, j):
            if 0 <= g < GROUPS:
                if j == 0:
                    h[g] = ring.tile([P, 2, H], BF16, name="h", bufs=HIDDEN_BUFS, align_bytes=64)
                dst = h[g][:, j, :].rearrange("c (u p d) -> c u p d", u=2, d=2)
                nc.vector.tensor_tensor(dst, by_pair(first_sums["a3", g, j]), sig[g, j][:], MULT)

        def turn(g):
            if 0 <= g < GROUPS:
                h_turned[g] = psum.tile([P, 2, 2, P], F32, name="h_turned", bufs=BANKS["h_turned"])
                for j in range(2):
                    for u in range(2):
                        h_pairs = h[g][:, j, :].bitcast(F32)[:, u * P : (u + 1) * P]
                        nc.tensor.transpose(h_turned[g][:, j, u, :], h_pairs, ident[:])

        def weave_h(g):
            if 0 <= g < GROUPS:
                h_woven[g] = ring.tile([P, 4 * C], BF16, name="h_woven", align_bytes=64)
                dst = h_woven[g][:].bitcast(F32).rearrange("p (j c u) -> p j c u", j=2, u=2)
                nc.scalar.copy(dst, h_turned[g][:].rearrange("p j u c -> p j c u"))

        def quantise_h(g):
            if 0 <= g < GROUPS:
                h_mx[g] = quantise(h_woven[g], "h")

        def second_product(g):
            if 0 <= g < GROUPS:
                e = min(g, E)
                codes, scales = h_mx[g]
                y[g] = psum.tile([P, 2, C], F32, name="y", bufs=BANKS["y"])
                for b in range(2):
                    cols = slice(b * P, (b + 1) * P)
                    if g < E:
                        nc.tensor.matmul_mx(
                            y[g][:, b, :],
                            lhsT=w2[e][:, 2 * b * P : 2 * (b + 1) * P].bitcast(FP4X4),
                            lhsT_scale=s2[:, e, cols],
                            rhs=codes[:].bitcast(FP8X4),
                            rhs_scale=scales[:],
                            start=True,
                            stop=True,
                        )
                    else:
                        nc.tensor.matmul_mx(
                            y[g][:, b, :],
                            lhsT=codes[:, cols].bitcast(FP8X4),
                            lhsT_scale=scales[:, cols],
                            rhs=w2[e].bitcast(FP4X4),
                            rhs_scale=s2[:, e, :],
                            start=True,
                            stop=True,
                        )

        shared = [keep.tile([P, 2, N], F32, name="shared%d" % half) for half in range(T // C)]

        def results_out(g):
            if 0 <= g < E:
                move = nc.vector.tensor_copy if g in RESULTS_ON_VECTOR else nc.scalar.copy
                for b in range(2):
                    move(y_sb[b][:, g * C : (g + 1) * C], y[g][:, b, :])
            elif E <= g < GROUPS:
                nc.scalar.copy(shared[g - E][:], y[g][:])

        for g in range(-3, GROUPS + 2):
            for j in range(2):
                sigmoid(g, j)
                hidden(g, j)
            turn(g)
            for words, plane, bank in ((w1, s1, "a1"), (w3, s3, "a3")):
                for j in range(2):
                    first_product(g + 1, j, words, plane, bank)
            weave_h(g - 1)
            quantise_h(g - 1)
            second_product(g - 1)
            results_out(g - 2)
            weave(g + 2)
            quantise_x(g + 2)
            for u in range(2):
                gather(g + 3, u)

        gates = keep.tile([P, TOP, T], F32, name="gates", tag="raw_left", align_bytes=64)
        nc.sync.dma_start(gates[:], gate[:, 0:P, :].rearrange("r p t -> p r t"))

        def gated_term(b, r, name, bufs):
            term = ring.tile([P, T], F32, name=name, bufs=bufs)
            nc.vector.tensor_tensor(term[:], y_sb[b][:].indirect(pos_sb[r][:]), gates[:, r, :], MULT)
            return term[:]

        chunks = [slice(c * P, (c + 1) * P) for c in range(T // P)]
        partial = []
        for b in range(2):
            terms = [gated_term(b, r, "term", 2 * (TOP - 1)) for r in range(TOP - 1)]
            turned = psum.tile([P, T], F32, name="a1", bufs=BANKS["a1"])
            steps = [(term, cols) for term in terms for cols in chunks]
            for n, (term, cols) in enumerate(steps):
                nc.tensor.matmul(turned[:, cols], term[:, cols], ident[:], start=n == 0, stop=n == len(steps) - 1, is_transpose=True)
            turned_sb = ring.tile([P, T], F32, name="turned_sb")
            nc.scalar.copy(turned_sb[:], turned[:])
            back = psum.tile([P, T], F32, name="a3", bufs=BANKS["a3"])
            steps = [(shared[c // 2][:, c % 2, b * P : (b + 1) * P], cols) for c, cols in enumerate(chunks)]
            steps = steps + [(turned_sb[:, cols], cols) for cols in chunks]
            for n, (src, cols) in enumerate(steps):
                nc.tensor.matmul(back[:, cols], src, ident[:], start=n == 0, stop=n == len(steps) - 1, is_transpose=True)
            partial.append(back)

        for b in range(2):
            last = gated_term(b, TOP - 1, "last", 2)
            total = ring.tile([P, T], F32, name="total")
            for cols in [slice(0, T)] if b == 0 else [slice(0, T // 2), slice(T // 2, T)]:
                nc.vector.tensor_tensor(total[:, cols], partial[b][:, cols], last[:, cols], ADD)
                nc.sync.dma_start(out[b * P : (b + 1) * P, cols], total[:, cols])
